import numpy as np
import ml_dtypes


def mxq(x, axis, fmt="e4m3"):
    dtype, down = {"e4m3": (ml_dtypes.float8_e4m3fn, 7), "e5m2": (ml_dtypes.float8_e5m2, 14)}[fmt]
    v = np.moveaxis(np.asarray(x, np.float32).astype(ml_dtypes.bfloat16).astype(np.float64), axis, -1)
    blocks = v.reshape(v.shape[:-1] + (-1, 32))
    amax = np.abs(blocks).max(-1, keepdims=True)
    byte = np.maximum(np.where(amax > 0, np.frexp(amax)[1] - 1 + 127, 0) - down, 1)
    scale = np.exp2(byte - 127.0)
    codes = (blocks / scale).astype(np.float32).astype(dtype).astype(np.float64)
    return np.moveaxis((codes * scale).reshape(v.shape), -1, axis)


WIDE = False


def mx_kscale(k):
    if not WIDE:
        return np.ones(k)
    levels = np.array([10, -10, 5, -5, 0])
    if k % 512:
        return np.exp2(np.random.permutation(np.resize(levels, k // 32))).repeat(32)
    a = np.empty((k // 512, 16))
    for p in range(k // 512):
        a[p, :8] = np.random.permutation(np.resize(levels, 8))
        for g in range(8):
            far = levels[np.abs(levels - a[p, g]) >= 10]
            a[p, g + 8] = far[np.random.randint(len(far))]
    return np.exp2(a.ravel()).repeat(32)


BF16 = ml_dtypes.bfloat16


def bf(x):
    return np.asarray(x, np.float32).astype(BF16)


def f64(x):
    return np.asarray(x).astype(np.float64)


E2M1 = np.array([0.0, 0.5, 1.0, 1.5, 2.0, 3.0, 4.0, 6.0, -0.0, -0.5, -1.0, -1.5, -2.0, -3.0, -4.0, -6.0])


def pack_weight(w, fmt):
    k, n = w.shape
    w = f64(bf(w)).reshape(k // 32, 32, n)
    amax = np.abs(w).max(1)
    if fmt == "e4m3":
        byte = np.frexp(amax)[1] - 1 + 127 - 7
    else:
        mant, ex = np.frexp(amax / 6.0)
        byte = np.where(mant > 0.5, ex, ex - 1) + 127
    byte = np.clip(np.where(amax > 0, byte, 1), 1, 254)
    scaled = (w * np.exp2(127.0 - byte)[:, None, :]).reshape(k, n).astype(np.float32)
    by_word = np.ascontiguousarray(scaled.reshape(k // 512, 128, 4, n).transpose(0, 1, 3, 2))
    if fmt == "e4m3":
        words = by_word.astype(ml_dtypes.float8_e4m3fn).view(np.uint8)
    else:
        c = by_word.astype(ml_dtypes.float4_e2m1fn).view(np.uint8) & 0xF
        words = c[..., 0::2] | (c[..., 1::2] << 4)
    return np.ascontiguousarray(words), np.ascontiguousarray(byte.astype(np.uint8).reshape(k // 512, 16, n))


def unpack_weight(words, scales, fmt):
    g, p, n, _ = words.shape
    if fmt == "e4m3":
        vals = np.ascontiguousarray(words).view(ml_dtypes.float8_e4m3fn).astype(np.float64)
    else:
        nib = np.empty((g, p, n, 4), np.uint8)
        nib[..., 0::2] = words & 0xF
        nib[..., 1::2] = words >> 4
        vals = E2M1[nib]
    vals = vals * np.repeat(np.exp2(scales.astype(np.float64) - 127.0), 8, axis=1)[..., None]
    return vals.transpose(0, 1, 3, 2).reshape(g * 512, n)
def pack4(w):
    words, scales = pack_weight(w, "e2m1")
    return words.reshape(words.shape[0], 128, -1), scales


def unpack4(words, scales):
    return unpack_weight(words.reshape(words.shape[0], 128, -1, 2), scales, "e2m1")


D, B = 2048, 512


def setup_inputs():
    s = mx_kscale(D)
    u = mx_kscale(D)
    w = np.random.standard_normal((D, D)) / np.sqrt(D) / s[:, None]
    w_words, w_scales = pack4(w)
    return {"x": bf(np.random.standard_normal((D, B)) * s[:, None]),
            "x_prev": bf(np.random.standard_normal((D, B)) * u[:, None]),
            "w_words": w_words,
            "w_scales": w_scales,
            "v": bf(np.random.standard_normal((D, D)) / np.sqrt(D) / u),
            "dg": bf((-1 + 0.3 * np.random.standard_normal(D)) / s),
            "mu": bf(0.7 + 0.2 * np.random.standard_normal(B)),
            "f": bf(np.random.standard_normal((D, B)))}


def reference(x, x_prev, w_words, w_scales, v, dg, mu, f):
    wt = unpack4(w_words, w_scales).T
    second = wt @ mxq(f64(x), 0, "e4m3")
    first = mxq(f64(v), 1, "e4m3") @ mxq(f64(x_prev), 0, "e4m3")
    y = second + first + f64(dg)[:, None] * f64(x)
    f_new = f64(f) + y * f64(mu)
    return y, f_new

@@ -1,0 +1,322 @@
+from contextlib import ExitStack
+
+import concourse.mybir as mybir
+from concourse.masks import make_identity
+
+D, B = 2048, 512
+FLOPS = 2 * 2 * D * D * B
+
+F32 = mybir.dt.float32
+BF16 = mybir.dt.bfloat16
+I32 = mybir.dt.int32
+U32 = mybir.dt.uint32
+U8 = mybir.dt.uint8
+FP8X4 = mybir.dt.float8_e4m3fn_x4
+FP4X4 = mybir.dt.float4_e2m1fn_x4
+ADD = mybir.AluOpType.add
+MULT = mybir.AluOpType.mult
+
+P = 128
+PACK = 4
+K_PASS = P * PACK
+PASSES = D // K_PASS
+TILES = D // P
+HEAD = 4
+FIRST_SORTED = 6
+VECTOR_COLS_PREV = 320
+VECTOR_COLS_X = 256
+W_CHUNKS = ((0, 4), (4, 6), (6, 8), (8, 12), (12, 16))
+ROW_CHUNKS = ((0, 2), (2, 4), (4, 8), (8, 12), (12, 16))
+F_CHUNKS = ((0, 4), (4, 8), (8, 12), (12, 16))
+OUT_CHUNKS = tuple((j, j + 2) for j in range(0, 14, 2)) + ((14, 15), (15, 16))
+
+
+def tile_chebyshev_two_step_filter_s1_kernel(tc, x, x_prev, w_words, w_scales, v, dg, mu, f, out_0, out_1):
+    nc = tc.nc
+
+    with ExitStack() as ctx:
+        keep = ctx.enter_context(tc.tile_pool(name="keep", bufs=1))
+        work = ctx.enter_context(tc.tile_pool(name="work", bufs=2))
+        psum = ctx.enter_context(tc.psum_pool(name="psum", bufs=4))
+        ctx.enter_context(tc.manual_schedule())
+
+        ident = keep.tile([P, P], F32, name="ident")
+        make_identity(nc, ident[:])
+
+        vec_rows = keep.tile([P, P], BF16, name="vec_rows")
+        nc.vector.memset(vec_rows[:], 0.0)
+        w_plane = keep.tile([P, PASSES, D], U8, name="w_plane", align_bytes=64)
+        nc.vector.memset(w_plane[:].rearrange("p g n -> p (g n)").bitcast(I32), 0)
+
+        raw, w_tile, x_rows, f_rows = {}, {}, {}, {}
+
+        def load_raw(key, src):
+            raw[key] = work.tile([P, PACK, B], BF16, name="raw", tag="raw", bufs=14)
+            nc.sync.dma_start(out=raw[key][:], in_=src)
+
+        def load_k_rows(name, src, g):
+            load_raw((name, g), src[K_PASS * g : K_PASS * (g + 1), :].rearrange("(p t) b -> p t b", t=PACK))
+
+        def load_v_head(g):
+            load_raw(("v_head", g), v[0 : HEAD * P, K_PASS * g : K_PASS * (g + 1)].rearrange("(j p) k -> p j k", p=P))
+
+        def load_v(j):
+            load_raw(("v", j), v[P * j : P * (j + 1), :].rearrange("p (g k) -> p g k", g=PASSES))
+
+        def load_w(c):
+            lo, hi = W_CHUNKS[c]
+            chunk = keep.tile([P, PASSES, 2 * P * (hi - lo)], U8, name="w_chunk%d" % c, align_bytes=64)
+            nc.sync.dma_start(
+                out=chunk[:].bitcast(I32),
+                in_=w_words[:, :, 2 * P * lo : 2 * P * hi].rearrange("g p n -> p g n").bitcast(I32),
+            )
+            for j in range(lo, hi):
+                w_tile[j] = chunk[:, :, 2 * P * (j - lo) : 2 * P * (j - lo + 1)]
+
+        def load_w_scales():
+            for q in range(4):
+                nc.sync.dma_start(
+                    out=w_plane[32 * q : 32 * q + 4, :, :].bitcast(I32),
+                    in_=w_scales[:, 4 * q : 4 * q + 4, :].rearrange("g r n -> r g n").bitcast(I32),
+                )
+
+        def load_rows(name, src, span, dest):
+            lo, hi = span
+            chunk = keep.tile([P, hi - lo, B], BF16, name="%s%d" % (name, lo))
+            nc.sync.dma_start(out=chunk[:], in_=src[P * lo : P * hi, :].rearrange("(j p) b -> p j b", p=P))
+            for j in range(lo, hi):
+                dest[j] = chunk[:, j - lo, :]
+
+        nc.sync.dma_start(out=vec_rows[0:TILES, :], in_=dg.rearrange("(j p) -> j p", p=P))
+        nc.sync.dma_start(out=vec_rows[TILES : TILES + 4, :], in_=mu.rearrange("(c p) -> c p", p=P))
+        for g in range(PASSES):
+            load_v_head(g)
+            load_k_rows("x_prev", x_prev, g)
+            if g == 1:
+                load_w_scales()
+        load_w(0)
+        for g in range(PASSES):
+            load_k_rows("x", x, g)
+        load_v(4)
+        load_rows("x_rows", x, ROW_CHUNKS[0], x_rows)
+        load_w(1)
+        load_v(5)
+        load_rows("x_rows", x, ROW_CHUNKS[1], x_rows)
+
+        vec_f32 = keep.tile([P, P], F32, name="vec_f32")
+        nc.vector.tensor_copy(out=vec_f32[:], in_=vec_rows[:])
+        bank = psum.tile([P, PACK, P], F32, name="turn", tag="turn")
+        nc.tensor.transpose(bank[:, 0, :], vec_f32[:], ident[:])
+        vec_cols = keep.tile([P, TILES + 4], F32, name="vec_cols")
+        nc.scalar.copy(out=vec_cols[:], in_=bank[:, 0, 0 : TILES + 4])
+        bank = psum.tile([P, PACK, P], F32, name="turn", tag="turn")
+        for c in range(4):
+            nc.tensor.transpose(bank[:, c, :], vec_cols[:, TILES + c : TILES + c + 1].to_broadcast([P, P]), ident[:])
+        mu_all = keep.tile([P, B], F32, name="mu_all")
+        nc.scalar.copy(out=mu_all[:], in_=bank[:].rearrange("p c n -> p (c n)"))
+
+        banks, grouped, codes, sorted_words = {}, {}, {}, {}
+
+        def presort(key):
+            words = raw[key][:].rearrange("p s k -> p (s k)").bitcast(F32)
+            sorted_words[key] = work.tile([P, 4, 2, P], F32, name="sorted_words", tag="sorted_words")
+            nc.scalar.copy(out=sorted_words[key][:], in_=words.rearrange("p (s m u) -> p s u m", s=4, u=2))
+
+        def turn(key):
+            words = raw[key][:].rearrange("p s k -> p (s k)").bitcast(F32)
+            banks[key] = []
+            for h in range(2):
+                bank = psum.tile([P, PACK, P], F32, name="turn", tag="turn")
+                banks[key].append(bank)
+                for q in range(4):
+                    s, u = 2 * h + q // 2, q % 2
+                    if key in sorted_words:
+                        src = sorted_words[key][:, s, u, :]
+                    else:
+                        src = words[:, 2 * P * s + u : 2 * P * (s + 1) : 2]
+                    nc.tensor.transpose(bank[:, q, :], src, ident[:])
+
+        def new_grouped(key):
+            grouped[key] = work.tile([P, 2048], BF16, name="grouped", tag="grouped", bufs=4, align_bytes=64)
+
+        def copy_out(key, h):
+            if h == 0:
+                new_grouped(key)
+            dst = grouped[key][:, 1024 * h : 1024 * (h + 1)].bitcast(F32).rearrange("p (s r u) -> p s r u", s=2, u=2)
+            nc.scalar.copy(out=dst, in_=banks[key][h][:].rearrange("p (s u) r -> p s r u", u=2))
+
+        def interleave(key, engine_copy, lo, hi):
+            dst = grouped[key][:, PACK * lo : PACK * hi].rearrange("p (c i t) -> p c t i", i=4, t=PACK)
+            engine_copy(out=dst, in_=raw[key][:, :, lo:hi].rearrange("p t (c i) -> p c t i", i=4))
+
+        def quantize(key, resident):
+            if resident:
+                words = keep.tile([P, B], U32, name="codes_%s%d" % key, align_bytes=64)
+                plane = keep.tile([P, B], U8, name="plane_%s%d" % key, align_bytes=64)
+            else:
+                words = work.tile([P, B], U32, name="v_codes", tag="v_codes", bufs=3, align_bytes=64)
+                plane = work.tile([P, B], U8, name="v_plane", tag="v_plane", bufs=3, align_bytes=64)
+            nc.vector.quantize_mx(out=words[:].bitcast(FP8X4), scales=plane[:], in_=grouped[key][:])
+            codes[key] = (words, plane)
+
+        acc = {}
+
+        def pass_v(j, g, key, s, start, stop):
+            words, plane = codes[key]
+            rhs, rhs_plane = codes[("x_prev", g)]
+            nc.tensor.matmul_mx(
+                out=acc[j][:],
+                lhsT=words[:, P * s : P * (s + 1)].bitcast(FP8X4),
+                lhsT_scale=plane[:, P * s : P * (s + 1)],
+                rhs=rhs[:].bitcast(FP8X4),
+                rhs_scale=rhs_plane[:],
+                start=start,
+                stop=stop,
+            )
+
+        def pass_w(j, g, start, stop):
+            rhs, rhs_plane = codes[("x", g)]
+            nc.tensor.matmul_mx(
+                out=acc[j][:],
+                lhsT=w_tile[j][:, g, :].bitcast(FP4X4),
+                lhsT_scale=w_plane[:, g, P * j : P * (j + 1)],
+                rhs=rhs[:].bitcast(FP8X4),
+                rhs_scale=rhs_plane[:],
+                start=start,
+                stop=stop,
+            )
+
+        def new_acc(j):
+            acc[j] = psum.tile([P, B], F32, name="acc", tag="acc")
+
+        y_out, f_out, chunk_of = {}, {}, {}
+
+        def finish_y(j, cols):
+            if j not in y_out:
+                lo, hi = [span for span in OUT_CHUNKS if span[0] == j][0]
+                y_chunk = work.tile([P, hi - lo, B], F32, name="y_chunk", tag="y_chunk", bufs=7)
+                f_chunk = work.tile([P, hi - lo, B], F32, name="f_chunk", tag="f_chunk", bufs=7)
+                chunk_of[hi - 1] = (lo, hi, y_chunk, f_chunk)
+                for i in range(lo, hi):
+                    y_out[i] = y_chunk[:, i - lo, :]
+                    f_out[i] = f_chunk[:, i - lo, :]
+            nc.vector.scalar_tensor_tensor(
+                out=y_out[j][:, cols], in0=x_rows[j][:, cols], scalar=vec_cols[:, j : j + 1], in1=acc[j][:, cols], op0=MULT, op1=ADD
+            )
+
+        def scale_y(j, cols):
+            nc.vector.tensor_tensor(out=f_out[j][:, cols], in0=y_out[j][:, cols], in1=mu_all[:, cols], op=MULT)
+
+        def add_f(j, cols):
+            nc.vector.tensor_tensor(out=f_out[j][:, cols], in0=f_out[j][:, cols], in1=f_rows[j][:, cols], op=ADD)
+
+        def store(j):
+            if j in chunk_of:
+                lo, hi, y_chunk, f_chunk = chunk_of[j]
+                nc.sync.dma_start(out=out_0[P * lo : P * hi, :].rearrange("(j p) b -> p j b", p=P), in_=y_chunk[:])
+                nc.sync.dma_start(out=out_1[P * lo : P * hi, :].rearrange("(j p) b -> p j b", p=P), in_=f_chunk[:])
+
+        whole = slice(0, B)
+
+        def prepare_prev(g):
+            key, prev = ("v_head", g), ("x_prev", g)
+            turn(key)
+            copy_out(key, 0)
+            new_grouped(prev)
+            interleave(prev, nc.vector.tensor_copy, 0, VECTOR_COLS_PREV)
+            interleave(prev, nc.scalar.copy, VECTOR_COLS_PREV, B)
+            copy_out(key, 1)
+            quantize(prev, True)
+            quantize(key, False)
+
+        def prepare_x(g):
+            key = ("x", g)
+            new_grouped(key)
+            interleave(key, nc.vector.tensor_copy, 0, VECTOR_COLS_X)
+            interleave(key, nc.scalar.copy, VECTOR_COLS_X, B)
+
+        for j in range(HEAD):
+            new_acc(j)
+        prepare_prev(0)
+        for g in range(PASSES):
+            if g + 1 < PASSES:
+                prepare_prev(g + 1)
+            for j in range(HEAD):
+                pass_v(j, g, ("v_head", g), j, g == 0, False)
+
+        load_v(6)
+        load_rows("f_rows", f, F_CHUNKS[0], f_rows)
+        load_w(2)
+        load_v(7)
+        load_rows("x_rows", x, ROW_CHUNKS[2], x_rows)
+        load_v(8)
+        load_w(3)
+        load_v(9)
+        load_rows("f_rows", f, F_CHUNKS[1], f_rows)
+
+        prepare_x(0)
+        for g in range(PASSES):
+            if g + 1 < PASSES:
+                prepare_x(g + 1)
+            quantize(("x", g), True)
+            if g + 1 == PASSES:
+                turn(("v", HEAD))
+                copy_out(("v", HEAD), 0)
+                copy_out(("v", HEAD), 1)
+            for j in range(HEAD):
+                pass_w(j, g, False, g + 1 == PASSES)
+
+        load_rows("x_rows", x, ROW_CHUNKS[3], x_rows)
+        load_v(10)
+        load_v(11)
+        load_rows("f_rows", f, F_CHUNKS[2], f_rows)
+        load_w(4)
+        load_v(12)
+        load_rows("x_rows", x, ROW_CHUNKS[4], x_rows)
+        load_v(13)
+        load_v(14)
+        load_v(15)
+        load_rows("f_rows", f, F_CHUNKS[3], f_rows)
+
+        finish_y(0, whole)
+        quantize(("v", HEAD), False)
+        for j in range(1, HEAD - 1):
+            finish_y(j, whole)
+
+        steps = [(step, j) for j in range(TILES) for step in (scale_y, add_f)]
+        done = [0]
+
+        def next_step(limit):
+            if done[0] <= limit:
+                step, j = steps[done[0]]
+                step(j, whole)
+                done[0] = done[0] + 1
+                if step is add_f:
+                    store(j)
+
+        for i in range(HEAD, TILES):
+            ahead = ("v", i + 1)
+            if i + 1 < TILES:
+                turn(ahead)
+                copy_out(ahead, 0)
+                copy_out(ahead, 1)
+            if FIRST_SORTED <= i + 2 < TILES:
+                presort(("v", i + 2))
+            finish_y(i - 1, whole)
+            next_step(2 * i - 3)
+            if i + 1 < TILES:
+                quantize(ahead, False)
+            next_step(2 * i - 2)
+            next_step(2 * i - 2)
+            new_acc(i)
+            for g in range(PASSES):
+                pass_w(i, g, g == 0, False)
+            for g in range(PASSES):
+                pass_v(i, g, ("v", i), g, False, g + 1 == PASSES)
+
+        last = TILES - 1
+        next_step(2 * last - 1)
+        for step in (finish_y, scale_y, add_f):
+            for half in range(2):
+                step(last, slice(half * B // 2, (half + 1) * B // 2))
+        store(last)

@@ -21,24 +21,43 @@ PACK = 4
 K_PASS = P * PACK
 PASSES = D // K_PASS
 TILES = D // P
-HEAD = 4
-FIRST_SORTED = 6
-VECTOR_COLS_PREV = 320
-VECTOR_COLS_X = 256
-W_CHUNKS = ((0, 4), (4, 6), (6, 8), (8, 12), (12, 16))
-ROW_CHUNKS = ((0, 2), (2, 4), (4, 8), (8, 12), (12, 16))
-F_CHUNKS = ((0, 4), (4, 8), (8, 12), (12, 16))
-OUT_CHUNKS = tuple((j, j + 2) for j in range(0, 14, 2)) + ((14, 15), (15, 16))
+LAST = TILES - 1
+MU_CHUNKS = B // P
+
+HEAD = 6
+EVEN_TURN_BANK = 6
+ODD_TURN_BANK = 1
+LATE_SUM_BANKS = (0, 3, 4, 5)
+UNSORTED = 2
+NEXT_TURN_AT = 3
+
+X_PREV_VECTOR_COLS = 448
+X_VECTOR_COLS = (512, 512, 256, 256)
+
+W_CHUNKS = ((0, 6), (6, 11), (11, 16))
+X_ROW_CHUNKS = ((0, 6), (6, 12), (12, 16))
+F_CHUNKS = ((0, 4), (4, 10), (10, 16))
+OUT_CHUNKS = ((0, 4), (4, 8), (8, 12), (12, 14), (14, 15), (15, 16))
+
+STREAM_BUFS = 11
+GROUPED_BUFS = 4
+V_CODE_BUFS = 5
 
 
 def tile_chebyshev_two_step_filter_s1_kernel(tc, x, x_prev, w_words, w_scales, v, dg, mu, f, out_0, out_1):
     nc = tc.nc
 
+    def tile_rows(src, lo, hi):
+        return src[P * lo : P * hi, :].rearrange("(j p) c -> p j c", p=P)
+
     with ExitStack() as ctx:
         keep = ctx.enter_context(tc.tile_pool(name="keep", bufs=1))
         work = ctx.enter_context(tc.tile_pool(name="work", bufs=2))
-        psum = ctx.enter_context(tc.psum_pool(name="psum", bufs=4))
+        psum = ctx.enter_context(tc.psum_pool(name="psum", bufs=1))
         ctx.enter_context(tc.manual_schedule())
+
+        def psum_bank(n, shape):
+            return psum.tile(shape, F32, name="bank%d" % n, tag="bank%d" % n)
 
         ident = keep.tile([P, P], F32, name="ident")
         make_identity(nc, ident[:])
@@ -48,160 +67,176 @@ def tile_chebyshev_two_step_filter_s1_kernel(tc, x, x_prev, w_words, w_scales, v
         w_plane = keep.tile([P, PASSES, D], U8, name="w_plane", align_bytes=64)
         nc.vector.memset(w_plane[:].rearrange("p g n -> p (g n)").bitcast(I32), 0)
 
-        raw, w_tile, x_rows, f_rows = {}, {}, {}, {}
+        raw, w_codes, x_rows, f_rows = {}, {}, {}, {}
 
-        def load_raw(key, src):
-            raw[key] = work.tile([P, PACK, B], BF16, name="raw", tag="raw", bufs=14)
+        def load_stream(key, src):
+            raw[key] = work.tile([P, PACK, B], BF16, name="raw", tag="raw", bufs=STREAM_BUFS)
             nc.sync.dma_start(out=raw[key][:], in_=src)
 
-        def load_k_rows(name, src, g):
-            load_raw((name, g), src[K_PASS * g : K_PASS * (g + 1), :].rearrange("(p t) b -> p t b", t=PACK))
-
-        def load_v_head(g):
-            load_raw(("v_head", g), v[0 : HEAD * P, K_PASS * g : K_PASS * (g + 1)].rearrange("(j p) k -> p j k", p=P))
-
         def load_v(j):
-            load_raw(("v", j), v[P * j : P * (j + 1), :].rearrange("p (g k) -> p g k", g=PASSES))
+            load_stream(("v", j), v[P * j : P * (j + 1), :].rearrange("p (g k) -> p g k", g=PASSES))
 
-        def load_w(c):
-            lo, hi = W_CHUNKS[c]
-            chunk = keep.tile([P, PASSES, 2 * P * (hi - lo)], U8, name="w_chunk%d" % c, align_bytes=64)
+        def load_k_rows(name, src, g):
+            load_stream((name, g), src[K_PASS * g : K_PASS * (g + 1), :].rearrange("(p t) c -> p t c", t=PACK))
+
+        def load_rows(name, src, span, dest):
+            lo, hi = span
+            chunk = keep.tile([P, hi - lo, B], BF16, name="%s%d" % (name, lo))
+            nc.sync.dma_start(out=chunk[:], in_=tile_rows(src, lo, hi))
+            for j in range(lo, hi):
+                dest[j] = chunk[:, j - lo, :]
+
+        def load_w(span):
+            lo, hi = span
+            chunk = keep.tile([P, PASSES, 2 * P * (hi - lo)], U8, name="w_chunk%d" % lo, align_bytes=64)
             nc.sync.dma_start(
                 out=chunk[:].bitcast(I32),
                 in_=w_words[:, :, 2 * P * lo : 2 * P * hi].rearrange("g p n -> p g n").bitcast(I32),
             )
             for j in range(lo, hi):
-                w_tile[j] = chunk[:, :, 2 * P * (j - lo) : 2 * P * (j - lo + 1)]
+                w_codes[j] = chunk[:, :, 2 * P * (j - lo) : 2 * P * (j - lo + 1)]
 
         def load_w_scales():
-            for q in range(4):
+            for r in range(4):
                 nc.sync.dma_start(
-                    out=w_plane[32 * q : 32 * q + 4, :, :].bitcast(I32),
-                    in_=w_scales[:, 4 * q : 4 * q + 4, :].rearrange("g r n -> r g n").bitcast(I32),
+                    out=w_plane[r:P:32, :, :].bitcast(I32),
+                    in_=w_scales[:, r:16:4, :].rearrange("g q n -> q g n").bitcast(I32),
                 )
 
-        def load_rows(name, src, span, dest):
-            lo, hi = span
-            chunk = keep.tile([P, hi - lo, B], BF16, name="%s%d" % (name, lo))
-            nc.sync.dma_start(out=chunk[:], in_=src[P * lo : P * hi, :].rearrange("(j p) b -> p j b", p=P))
-            for j in range(lo, hi):
-                dest[j] = chunk[:, j - lo, :]
-
-        nc.sync.dma_start(out=vec_rows[0:TILES, :], in_=dg.rearrange("(j p) -> j p", p=P))
-        nc.sync.dma_start(out=vec_rows[TILES : TILES + 4, :], in_=mu.rearrange("(c p) -> c p", p=P))
-        for g in range(PASSES):
-            load_v_head(g)
-            load_k_rows("x_prev", x_prev, g)
-            if g == 1:
-                load_w_scales()
-        load_w(0)
-        for g in range(PASSES):
-            load_k_rows("x", x, g)
+        load_v(0)
+        nc.sync.dma_start(out=vec_rows[0:MU_CHUNKS, :], in_=mu.rearrange("(c p) -> c p", p=P))
+        nc.sync.dma_start(out=vec_rows[MU_CHUNKS : MU_CHUNKS + TILES, :], in_=dg.rearrange("(j p) -> j p", p=P))
+        load_k_rows("x_prev", x_prev, 0)
+        load_v(1)
+        load_k_rows("x_prev", x_prev, 1)
+        load_k_rows("x_prev", x_prev, 2)
+        load_v(2)
+        load_k_rows("x_prev", x_prev, 3)
+        load_v(3)
         load_v(4)
-        load_rows("x_rows", x, ROW_CHUNKS[0], x_rows)
-        load_w(1)
+        load_k_rows("x", x, 0)
         load_v(5)
-        load_rows("x_rows", x, ROW_CHUNKS[1], x_rows)
 
         vec_f32 = keep.tile([P, P], F32, name="vec_f32")
         nc.vector.tensor_copy(out=vec_f32[:], in_=vec_rows[:])
-        bank = psum.tile([P, PACK, P], F32, name="turn", tag="turn")
-        nc.tensor.transpose(bank[:, 0, :], vec_f32[:], ident[:])
-        vec_cols = keep.tile([P, TILES + 4], F32, name="vec_cols")
-        nc.scalar.copy(out=vec_cols[:], in_=bank[:, 0, 0 : TILES + 4])
-        bank = psum.tile([P, PACK, P], F32, name="turn", tag="turn")
-        for c in range(4):
-            nc.tensor.transpose(bank[:, c, :], vec_cols[:, TILES + c : TILES + c + 1].to_broadcast([P, P]), ident[:])
+        vec_bank = psum_bank(0, [P, P])
+        nc.tensor.transpose(vec_bank[:], vec_f32[:], ident[:])
+        vec_cols = keep.tile([P, MU_CHUNKS + TILES], F32, name="vec_cols")
+        nc.scalar.copy(out=vec_cols[:], in_=vec_bank[:, 0 : MU_CHUNKS + TILES])
+        mu_bank = psum_bank(1, [P, MU_CHUNKS, P])
+        for c in range(MU_CHUNKS):
+            nc.tensor.transpose(mu_bank[:, c, :], vec_cols[:, c : c + 1].to_broadcast([P, P]), ident[:])
         mu_all = keep.tile([P, B], F32, name="mu_all")
-        nc.scalar.copy(out=mu_all[:], in_=bank[:].rearrange("p c n -> p (c n)"))
+        nc.scalar.copy(out=mu_all[:], in_=mu_bank[:].rearrange("p c n -> p (c n)"))
 
-        banks, grouped, codes, sorted_words = {}, {}, {}, {}
+        sorted_words, turned, grouped, codes = {}, {}, {}, {}
 
-        def presort(key):
-            words = raw[key][:].rearrange("p s k -> p (s k)").bitcast(F32)
-            sorted_words[key] = work.tile([P, 4, 2, P], F32, name="sorted_words", tag="sorted_words")
-            nc.scalar.copy(out=sorted_words[key][:], in_=words.rearrange("p (s m u) -> p s u m", s=4, u=2))
+        def v_words(j):
+            return raw[("v", j)][:].rearrange("p g k -> p (g k)").bitcast(F32)
 
-        def turn(key):
-            words = raw[key][:].rearrange("p s k -> p (s k)").bitcast(F32)
-            banks[key] = []
+        def sort_words(j):
+            sorted_words[j] = work.tile([P, PASSES, 2, P], F32, name="sorted_words", tag="sorted_words")
+            nc.scalar.copy(out=sorted_words[j][:], in_=v_words(j).rearrange("p (g m u) -> p g u m", g=PASSES, u=2))
+
+        def turn(j):
+            first_bank = ODD_TURN_BANK if j > HEAD + 1 and j % 2 == 1 else EVEN_TURN_BANK
+            turned[j] = []
             for h in range(2):
-                bank = psum.tile([P, PACK, P], F32, name="turn", tag="turn")
-                banks[key].append(bank)
-                for q in range(4):
-                    s, u = 2 * h + q // 2, q % 2
-                    if key in sorted_words:
-                        src = sorted_words[key][:, s, u, :]
-                    else:
-                        src = words[:, 2 * P * s + u : 2 * P * (s + 1) : 2]
-                    nc.tensor.transpose(bank[:, q, :], src, ident[:])
+                bank = psum_bank(first_bank + h, [P, 4, P])
+                turned[j].append(bank)
+                for g in (2 * h, 2 * h + 1):
+                    for u in range(2):
+                        if j < UNSORTED:
+                            src = v_words(j)[:, 2 * P * g + u : 2 * P * (g + 1) : 2]
+                        else:
+                            src = sorted_words[j][:, g, u, :]
+                        nc.tensor.transpose(bank[:, 2 * (g % 2) + u, :], src, ident[:])
 
         def new_grouped(key):
-            grouped[key] = work.tile([P, 2048], BF16, name="grouped", tag="grouped", bufs=4, align_bytes=64)
+            grouped[key] = work.tile([P, PACK * B], BF16, name="grouped", tag="grouped", bufs=GROUPED_BUFS, align_bytes=64)
 
-        def copy_out(key, h):
+        def copy_out(j, h):
             if h == 0:
-                new_grouped(key)
-            dst = grouped[key][:, 1024 * h : 1024 * (h + 1)].bitcast(F32).rearrange("p (s r u) -> p s r u", s=2, u=2)
-            nc.scalar.copy(out=dst, in_=banks[key][h][:].rearrange("p (s u) r -> p s r u", u=2))
+                new_grouped(("v", j))
+            half = grouped[("v", j)][:, 2 * B * h : 2 * B * (h + 1)]
+            nc.scalar.copy(
+                out=half.bitcast(F32).rearrange("p (g r u) -> p g r u", g=2, u=2),
+                in_=turned[j][h][:].rearrange("p (g u) r -> p g r u", u=2),
+            )
 
-        def interleave(key, engine_copy, lo, hi):
-            dst = grouped[key][:, PACK * lo : PACK * hi].rearrange("p (c i t) -> p c t i", i=4, t=PACK)
-            engine_copy(out=dst, in_=raw[key][:, :, lo:hi].rearrange("p t (c i) -> p c t i", i=4))
+        def turn_and_copy(j):
+            turn(j)
+            copy_out(j, 0)
+            copy_out(j, 1)
 
-        def quantize(key, resident):
-            if resident:
+        def interleave(key, vector_cols):
+            new_grouped(key)
+            for engine_copy, lo, hi in ((nc.vector.tensor_copy, 0, vector_cols), (nc.scalar.copy, vector_cols, B)):
+                if lo < hi:
+                    engine_copy(
+                        out=grouped[key][:, PACK * lo : PACK * hi].rearrange("p (c i t) -> p c t i", i=4, t=PACK),
+                        in_=raw[key][:, :, lo:hi].rearrange("p t (c i) -> p c t i", i=4),
+                    )
+
+        def quantize(key):
+            if key[0] == "v":
+                words = work.tile([P, B], U32, name="v_codes", tag="v_codes", bufs=V_CODE_BUFS, align_bytes=64)
+                plane = work.tile([P, B], U8, name="v_plane", tag="v_plane", bufs=V_CODE_BUFS, align_bytes=64)
+            else:
                 words = keep.tile([P, B], U32, name="codes_%s%d" % key, align_bytes=64)
                 plane = keep.tile([P, B], U8, name="plane_%s%d" % key, align_bytes=64)
-            else:
-                words = work.tile([P, B], U32, name="v_codes", tag="v_codes", bufs=3, align_bytes=64)
-                plane = work.tile([P, B], U8, name="v_plane", tag="v_plane", bufs=3, align_bytes=64)
             nc.vector.quantize_mx(out=words[:].bitcast(FP8X4), scales=plane[:], in_=grouped[key][:])
             codes[key] = (words, plane)
 
         acc = {}
 
-        def pass_v(j, g, key, s, start, stop):
-            words, plane = codes[key]
-            rhs, rhs_plane = codes[("x_prev", g)]
+        def pass_v(j, g, start, stop):
+            words, plane = codes[("v", j)]
+            rhs_words, rhs_plane = codes[("x_prev", g)]
             nc.tensor.matmul_mx(
                 out=acc[j][:],
-                lhsT=words[:, P * s : P * (s + 1)].bitcast(FP8X4),
-                lhsT_scale=plane[:, P * s : P * (s + 1)],
-                rhs=rhs[:].bitcast(FP8X4),
+                lhsT=words[:, P * g : P * (g + 1)].bitcast(FP8X4),
+                lhsT_scale=plane[:, P * g : P * (g + 1)],
+                rhs=rhs_words[:].bitcast(FP8X4),
                 rhs_scale=rhs_plane[:],
                 start=start,
                 stop=stop,
             )
 
         def pass_w(j, g, start, stop):
-            rhs, rhs_plane = codes[("x", g)]
+            rhs_words, rhs_plane = codes[("x", g)]
             nc.tensor.matmul_mx(
                 out=acc[j][:],
-                lhsT=w_tile[j][:, g, :].bitcast(FP4X4),
+                lhsT=w_codes[j][:, g, :].bitcast(FP4X4),
                 lhsT_scale=w_plane[:, g, P * j : P * (j + 1)],
-                rhs=rhs[:].bitcast(FP8X4),
+                rhs=rhs_words[:].bitcast(FP8X4),
                 rhs_scale=rhs_plane[:],
                 start=start,
                 stop=stop,
             )
 
-        def new_acc(j):
-            acc[j] = psum.tile([P, B], F32, name="acc", tag="acc")
+        def head_passes_v(tiles, groups):
+            for j in tiles:
+                for g in groups:
+                    pass_v(j, g, g == 0, False)
 
-        y_out, f_out, chunk_of = {}, {}, {}
+        y_out, f_out, chunk_ending_at = {}, {}, {}
+        for lo, hi in OUT_CHUNKS:
+            y_chunk = keep.tile([P, hi - lo, B], F32, name="y_chunk%d" % lo)
+            f_chunk = keep.tile([P, hi - lo, B], F32, name="f_chunk%d" % lo)
+            chunk_ending_at[hi - 1] = (lo, hi, y_chunk, f_chunk)
+            for j in range(lo, hi):
+                y_out[j] = y_chunk[:, j - lo, :]
+                f_out[j] = f_chunk[:, j - lo, :]
 
         def finish_y(j, cols):
-            if j not in y_out:
-                lo, hi = [span for span in OUT_CHUNKS if span[0] == j][0]
-                y_chunk = work.tile([P, hi - lo, B], F32, name="y_chunk", tag="y_chunk", bufs=7)
-                f_chunk = work.tile([P, hi - lo, B], F32, name="f_chunk", tag="f_chunk", bufs=7)
-                chunk_of[hi - 1] = (lo, hi, y_chunk, f_chunk)
-                for i in range(lo, hi):
-                    y_out[i] = y_chunk[:, i - lo, :]
-                    f_out[i] = f_chunk[:, i - lo, :]
             nc.vector.scalar_tensor_tensor(
-                out=y_out[j][:, cols], in0=x_rows[j][:, cols], scalar=vec_cols[:, j : j + 1], in1=acc[j][:, cols], op0=MULT, op1=ADD
+                out=y_out[j][:, cols],
+                in0=x_rows[j][:, cols],
+                scalar=vec_cols[:, MU_CHUNKS + j : MU_CHUNKS + j + 1],
+                in1=acc[j][:, cols],
+                op0=MULT,
+                op1=ADD,
             )
 
         def scale_y(j, cols):
@@ -210,113 +245,119 @@ def tile_chebyshev_two_step_filter_s1_kernel(tc, x, x_prev, w_words, w_scales, v
         def add_f(j, cols):
             nc.vector.tensor_tensor(out=f_out[j][:, cols], in0=f_out[j][:, cols], in1=f_rows[j][:, cols], op=ADD)
 
-        def store(j):
-            if j in chunk_of:
-                lo, hi, y_chunk, f_chunk = chunk_of[j]
-                nc.sync.dma_start(out=out_0[P * lo : P * hi, :].rearrange("(j p) b -> p j b", p=P), in_=y_chunk[:])
-                nc.sync.dma_start(out=out_1[P * lo : P * hi, :].rearrange("(j p) b -> p j b", p=P), in_=f_chunk[:])
+        def store_chunk_ending_at(j):
+            if j in chunk_ending_at:
+                lo, hi, y_chunk, f_chunk = chunk_ending_at[j]
+                nc.sync.dma_start(out=tile_rows(out_0, lo, hi), in_=y_chunk[:])
+                nc.sync.dma_start(out=tile_rows(out_1, lo, hi), in_=f_chunk[:])
 
         whole = slice(0, B)
+        pending = [(step, j) for j in range(LAST) for step in (scale_y, add_f)]
 
-        def prepare_prev(g):
-            key, prev = ("v_head", g), ("x_prev", g)
-            turn(key)
-            copy_out(key, 0)
-            new_grouped(prev)
-            interleave(prev, nc.vector.tensor_copy, 0, VECTOR_COLS_PREV)
-            interleave(prev, nc.scalar.copy, VECTOR_COLS_PREV, B)
-            copy_out(key, 1)
-            quantize(prev, True)
-            quantize(key, False)
-
-        def prepare_x(g):
-            key = ("x", g)
-            new_grouped(key)
-            interleave(key, nc.vector.tensor_copy, 0, VECTOR_COLS_X)
-            interleave(key, nc.scalar.copy, VECTOR_COLS_X, B)
+        def run_pending(at_most, newest_tile):
+            for step, j in pending[:at_most]:
+                if j <= newest_tile:
+                    pending.remove((step, j))
+                    step(j, whole)
+                    if step is add_f:
+                        store_chunk_ending_at(j)
 
         for j in range(HEAD):
-            new_acc(j)
-        prepare_prev(0)
-        for g in range(PASSES):
-            if g + 1 < PASSES:
-                prepare_prev(g + 1)
-            for j in range(HEAD):
-                pass_v(j, g, ("v_head", g), j, g == 0, False)
+            acc[j] = psum_bank(j, [P, B])
+        turn(0)
+        copy_out(0, 0)
+        interleave(("x_prev", 0), X_PREV_VECTOR_COLS)
+        copy_out(0, 1)
+        turn(1)
+        interleave(("x_prev", 1), X_PREV_VECTOR_COLS)
+        copy_out(1, 0)
+        copy_out(1, 1)
+        for s in range(2):
+            quantize(("x_prev", s))
+            quantize(("v", s))
+        for g in range(1, PASSES):
+            load_k_rows("x", x, g)
+        load_w_scales()
+        load_w(W_CHUNKS[0])
+        interleave(("x_prev", 2), X_PREV_VECTOR_COLS)
+        sort_words(2)
+        head_passes_v((0, 1), (0, 1))
+        quantize(("x_prev", 2))
+        interleave(("x_prev", 3), X_PREV_VECTOR_COLS)
+        sort_words(3)
+        turn_and_copy(2)
+        head_passes_v((0, 1), (2,))
+        quantize(("x_prev", 3))
+        quantize(("v", 2))
+
+        for j in range(2, HEAD):
+            if j + 2 < HEAD:
+                sort_words(j + 2)
+            if j + 1 < HEAD:
+                turn_and_copy(j + 1)
+            interleave(("x", j - 2), X_VECTOR_COLS[j - 2])
+            if j + 1 < HEAD:
+                quantize(("v", j + 1))
+            quantize(("x", j - 2))
+            if j == 2:
+                head_passes_v((0, 1), (3,))
+            head_passes_v((j,), range(PASSES))
 
         load_v(6)
-        load_rows("f_rows", f, F_CHUNKS[0], f_rows)
-        load_w(2)
+        load_rows("x_rows", x, X_ROW_CHUNKS[0], x_rows)
         load_v(7)
-        load_rows("x_rows", x, ROW_CHUNKS[2], x_rows)
+        load_w(W_CHUNKS[1])
+        load_rows("f_rows", f, F_CHUNKS[0], f_rows)
         load_v(8)
-        load_w(3)
+        load_rows("x_rows", x, X_ROW_CHUNKS[1], x_rows)
         load_v(9)
         load_rows("f_rows", f, F_CHUNKS[1], f_rows)
+        load_v(10)
+        load_w(W_CHUNKS[2])
+        load_v(11)
+        load_rows("x_rows", x, X_ROW_CHUNKS[2], x_rows)
+        load_v(12)
+        load_rows("f_rows", f, F_CHUNKS[2], f_rows)
+        for j in range(13, TILES):
+            load_v(j)
 
-        prepare_x(0)
-        for g in range(PASSES):
-            if g + 1 < PASSES:
-                prepare_x(g + 1)
-            quantize(("x", g), True)
-            if g + 1 == PASSES:
-                turn(("v", HEAD))
-                copy_out(("v", HEAD), 0)
-                copy_out(("v", HEAD), 1)
-            for j in range(HEAD):
+        sort_words(HEAD)
+        for j in range(HEAD):
+            if j == NEXT_TURN_AT:
+                turn_and_copy(HEAD)
+                sort_words(HEAD + 1)
+            if j > 0:
+                finish_y(j - 1, whole)
+                run_pending(1, j - 2)
+            if j == NEXT_TURN_AT + 1:
+                quantize(("v", HEAD))
+            for g in range(PASSES):
                 pass_w(j, g, False, g + 1 == PASSES)
 
-        load_rows("x_rows", x, ROW_CHUNKS[3], x_rows)
-        load_v(10)
-        load_v(11)
-        load_rows("f_rows", f, F_CHUNKS[2], f_rows)
-        load_w(4)
-        load_v(12)
-        load_rows("x_rows", x, ROW_CHUNKS[4], x_rows)
-        load_v(13)
-        load_v(14)
-        load_v(15)
-        load_rows("f_rows", f, F_CHUNKS[3], f_rows)
-
-        finish_y(0, whole)
-        quantize(("v", HEAD), False)
-        for j in range(1, HEAD - 1):
-            finish_y(j, whole)
-
-        steps = [(step, j) for j in range(TILES) for step in (scale_y, add_f)]
-        done = [0]
-
-        def next_step(limit):
-            if done[0] <= limit:
-                step, j = steps[done[0]]
-                step(j, whole)
-                done[0] = done[0] + 1
-                if step is add_f:
-                    store(j)
-
-        for i in range(HEAD, TILES):
-            ahead = ("v", i + 1)
-            if i + 1 < TILES:
-                turn(ahead)
-                copy_out(ahead, 0)
-                copy_out(ahead, 1)
-            if FIRST_SORTED <= i + 2 < TILES:
-                presort(("v", i + 2))
-            finish_y(i - 1, whole)
-            next_step(2 * i - 3)
-            if i + 1 < TILES:
-                quantize(ahead, False)
-            next_step(2 * i - 2)
-            next_step(2 * i - 2)
-            new_acc(i)
+        for j in range(HEAD, TILES):
+            if j == HEAD:
+                turn_and_copy(j + 1)
+                sort_words(j + 2)
+                sort_words(j + 3)
+            elif j % 2 == 1 and j < LAST:
+                turn_and_copy(j + 1)
+                turn_and_copy(j + 2)
+                if j + 3 < TILES:
+                    sort_words(j + 3)
+                    sort_words(j + 4)
+            finish_y(j - 1, whole)
+            run_pending(1, j - 2)
+            if j < LAST:
+                quantize(("v", j + 1))
+            run_pending(2, j - 1)
+            acc[j] = psum_bank(LATE_SUM_BANKS[(j - HEAD) % len(LATE_SUM_BANKS)], [P, B])
             for g in range(PASSES):
-                pass_w(i, g, g == 0, False)
+                pass_w(j, g, g == 0, False)
             for g in range(PASSES):
-                pass_v(i, g, ("v", i), g, False, g + 1 == PASSES)
+                pass_v(j, g, False, g + 1 == PASSES)
 
-        last = TILES - 1
-        next_step(2 * last - 1)
+        assert not pending
         for step in (finish_y, scale_y, add_f):
             for half in range(2):
-                step(last, slice(half * B // 2, (half + 1) * B // 2))
-        store(last)
+                step(LAST, slice(half * B // 2, (half + 1) * B // 2))
+        store_chunk_ending_at(LAST)

from contextlib import ExitStack

import concourse.mybir as mybir
from concourse.masks import make_identity

D, B = 2048, 512
FLOPS = 2 * 2 * D * D * B

F32 = mybir.dt.float32
BF16 = mybir.dt.bfloat16
I32 = mybir.dt.int32
U32 = mybir.dt.uint32
U8 = mybir.dt.uint8
FP8X4 = mybir.dt.float8_e4m3fn_x4
FP4X4 = mybir.dt.float4_e2m1fn_x4
ADD = mybir.AluOpType.add
MULT = mybir.AluOpType.mult

P = 128
PACK = 4
K_PASS = P * PACK
PASSES = D // K_PASS
TILES = D // P
LAST = TILES - 1
MU_CHUNKS = B // P

HEAD = 6
EVEN_TURN_BANK = 6
ODD_TURN_BANK = 1
LATE_SUM_BANKS = (0, 3, 4, 5)
UNSORTED = 2
NEXT_TURN_AT = 3

X_PREV_VECTOR_COLS = 448
X_VECTOR_COLS = (512, 512, 256, 256)

W_CHUNKS = ((0, 6), (6, 11), (11, 16))
X_ROW_CHUNKS = ((0, 6), (6, 12), (12, 16))
F_CHUNKS = ((0, 4), (4, 10), (10, 16))
OUT_CHUNKS = ((0, 4), (4, 8), (8, 12), (12, 14), (14, 15), (15, 16))

STREAM_BUFS = 11
GROUPED_BUFS = 4
V_CODE_BUFS = 5


def tile_chebyshev_two_step_filter_s1_kernel(tc, x, x_prev, w_words, w_scales, v, dg, mu, f, out_0, out_1):
    nc = tc.nc

    def tile_rows(src, lo, hi):
        return src[P * lo : P * hi, :].rearrange("(j p) c -> p j c", p=P)

    with ExitStack() as ctx:
        keep = ctx.enter_context(tc.tile_pool(name="keep", bufs=1))
        work = ctx.enter_context(tc.tile_pool(name="work", bufs=2))
        psum = ctx.enter_context(tc.psum_pool(name="psum", bufs=1))
        ctx.enter_context(tc.manual_schedule())

        def psum_bank(n, shape):
            return psum.tile(shape, F32, name="bank%d" % n, tag="bank%d" % n)

        ident = keep.tile([P, P], F32, name="ident")
        make_identity(nc, ident[:])

        vec_rows = keep.tile([P, P], BF16, name="vec_rows")
        nc.vector.memset(vec_rows[:], 0.0)
        w_plane = keep.tile([P, PASSES, D], U8, name="w_plane", align_bytes=64)
        nc.vector.memset(w_plane[:].rearrange("p g n -> p (g n)").bitcast(I32), 0)

        raw, w_codes, x_rows, f_rows = {}, {}, {}, {}

        def load_stream(key, src):
            raw[key] = work.tile([P, PACK, B], BF16, name="raw", tag="raw", bufs=STREAM_BUFS)
            nc.sync.dma_start(out=raw[key][:], in_=src)

        def load_v(j):
            load_stream(("v", j), v[P * j : P * (j + 1), :].rearrange("p (g k) -> p g k", g=PASSES))

        def load_k_rows(name, src, g):
            load_stream((name, g), src[K_PASS * g : K_PASS * (g + 1), :].rearrange("(p t) c -> p t c", t=PACK))

        def load_rows(name, src, span, dest):
            lo, hi = span
            chunk = keep.tile([P, hi - lo, B], BF16, name="%s%d" % (name, lo))
            nc.sync.dma_start(out=chunk[:], in_=tile_rows(src, lo, hi))
            for j in range(lo, hi):
                dest[j] = chunk[:, j - lo, :]

        def load_w(span):
            lo, hi = span
            chunk = keep.tile([P, PASSES, 2 * P * (hi - lo)], U8, name="w_chunk%d" % lo, align_bytes=64)
            nc.sync.dma_start(
                out=chunk[:].bitcast(I32),
                in_=w_words[:, :, 2 * P * lo : 2 * P * hi].rearrange("g p n -> p g n").bitcast(I32),
            )
            for j in range(lo, hi):
                w_codes[j] = chunk[:, :, 2 * P * (j - lo) : 2 * P * (j - lo + 1)]

        def load_w_scales():
            for r in range(4):
                nc.sync.dma_start(
                    out=w_plane[r:P:32, :, :].bitcast(I32),
                    in_=w_scales[:, r:16:4, :].rearrange("g q n -> q g n").bitcast(I32),
                )

        load_v(0)
        nc.sync.dma_start(out=vec_rows[0:MU_CHUNKS, :], in_=mu.rearrange("(c p) -> c p", p=P))
        nc.sync.dma_start(out=vec_rows[MU_CHUNKS : MU_CHUNKS + TILES, :], in_=dg.rearrange("(j p) -> j p", p=P))
        load_k_rows("x_prev", x_prev, 0)
        load_v(1)
        load_k_rows("x_prev", x_prev, 1)
        load_k_rows("x_prev", x_prev, 2)
        load_v(2)
        load_k_rows("x_prev", x_prev, 3)
        load_v(3)
        load_v(4)
        load_k_rows("x", x, 0)
        load_v(5)

        vec_f32 = keep.tile([P, P], F32, name="vec_f32")
        nc.vector.tensor_copy(out=vec_f32[:], in_=vec_rows[:])
        vec_bank = psum_bank(0, [P, P])
        nc.tensor.transpose(vec_bank[:], vec_f32[:], ident[:])
        vec_cols = keep.tile([P, MU_CHUNKS + TILES], F32, name="vec_cols")
        nc.scalar.copy(out=vec_cols[:], in_=vec_bank[:, 0 : MU_CHUNKS + TILES])
        mu_bank = psum_bank(1, [P, MU_CHUNKS, P])
        for c in range(MU_CHUNKS):
            nc.tensor.transpose(mu_bank[:, c, :], vec_cols[:, c : c + 1].to_broadcast([P, P]), ident[:])
        mu_all = keep.tile([P, B], F32, name="mu_all")
        nc.scalar.copy(out=mu_all[:], in_=mu_bank[:].rearrange("p c n -> p (c n)"))

        sorted_words, turned, grouped, codes = {}, {}, {}, {}

        def v_words(j):
            return raw[("v", j)][:].rearrange("p g k -> p (g k)").bitcast(F32)

        def sort_words(j):
            sorted_words[j] = work.tile([P, PASSES, 2, P], F32, name="sorted_words", tag="sorted_words")
            nc.scalar.copy(out=sorted_words[j][:], in_=v_words(j).rearrange("p (g m u) -> p g u m", g=PASSES, u=2))

        def turn(j):
            first_bank = ODD_TURN_BANK if j > HEAD + 1 and j % 2 == 1 else EVEN_TURN_BANK
            turned[j] = []
            for h in range(2):
                bank = psum_bank(first_bank + h, [P, 4, P])
                turned[j].append(bank)
                for g in (2 * h, 2 * h + 1):
                    for u in range(2):
                        if j < UNSORTED:
                            src = v_words(j)[:, 2 * P * g + u : 2 * P * (g + 1) : 2]
                        else:
                            src = sorted_words[j][:, g, u, :]
                        nc.tensor.transpose(bank[:, 2 * (g % 2) + u, :], src, ident[:])

        def new_grouped(key):
            grouped[key] = work.tile([P, PACK * B], BF16, name="grouped", tag="grouped", bufs=GROUPED_BUFS, align_bytes=64)

        def copy_out(j, h):
            if h == 0:
                new_grouped(("v", j))
            half = grouped[("v", j)][:, 2 * B * h : 2 * B * (h + 1)]
            nc.scalar.copy(
                out=half.bitcast(F32).rearrange("p (g r u) -> p g r u", g=2, u=2),
                in_=turned[j][h][:].rearrange("p (g u) r -> p g r u", u=2),
            )

        def turn_and_copy(j):
            turn(j)
            copy_out(j, 0)
            copy_out(j, 1)

        def interleave(key, vector_cols):
            new_grouped(key)
            for engine_copy, lo, hi in ((nc.vector.tensor_copy, 0, vector_cols), (nc.scalar.copy, vector_cols, B)):
                if lo < hi:
                    engine_copy(
                        out=grouped[key][:, PACK * lo : PACK * hi].rearrange("p (c i t) -> p c t i", i=4, t=PACK),
                        in_=raw[key][:, :, lo:hi].rearrange("p t (c i) -> p c t i", i=4),
                    )

        def quantize(key):
            if key[0] == "v":
                words = work.tile([P, B], U32, name="v_codes", tag="v_codes", bufs=V_CODE_BUFS, align_bytes=64)
                plane = work.tile([P, B], U8, name="v_plane", tag="v_plane", bufs=V_CODE_BUFS, align_bytes=64)
            else:
                words = keep.tile([P, B], U32, name="codes_%s%d" % key, align_bytes=64)
                plane = keep.tile([P, B], U8, name="plane_%s%d" % key, align_bytes=64)
            nc.vector.quantize_mx(out=words[:].bitcast(FP8X4), scales=plane[:], in_=grouped[key][:])
            codes[key] = (words, plane)

        acc = {}

        def pass_v(j, g, start, stop):
            words, plane = codes[("v", j)]
            rhs_words, rhs_plane = codes[("x_prev", g)]
            nc.tensor.matmul_mx(
                out=acc[j][:],
                lhsT=words[:, P * g : P * (g + 1)].bitcast(FP8X4),
                lhsT_scale=plane[:, P * g : P * (g + 1)],
                rhs=rhs_words[:].bitcast(FP8X4),
                rhs_scale=rhs_plane[:],
                start=start,
                stop=stop,
            )

        def pass_w(j, g, start, stop):
            rhs_words, rhs_plane = codes[("x", g)]
            nc.tensor.matmul_mx(
                out=acc[j][:],
                lhsT=w_codes[j][:, g, :].bitcast(FP4X4),
                lhsT_scale=w_plane[:, g, P * j : P * (j + 1)],
                rhs=rhs_words[:].bitcast(FP8X4),
                rhs_scale=rhs_plane[:],
                start=start,
                stop=stop,
            )

        def head_passes_v(tiles, groups):
            for j in tiles:
                for g in groups:
                    pass_v(j, g, g == 0, False)

        y_out, f_out, chunk_ending_at = {}, {}, {}
        for lo, hi in OUT_CHUNKS:
            y_chunk = keep.tile([P, hi - lo, B], F32, name="y_chunk%d" % lo)
            f_chunk = keep.tile([P, hi - lo, B], F32, name="f_chunk%d" % lo)
            chunk_ending_at[hi - 1] = (lo, hi, y_chunk, f_chunk)
            for j in range(lo, hi):
                y_out[j] = y_chunk[:, j - lo, :]
                f_out[j] = f_chunk[:, j - lo, :]

        def finish_y(j, cols):
            nc.vector.scalar_tensor_tensor(
                out=y_out[j][:, cols],
                in0=x_rows[j][:, cols],
                scalar=vec_cols[:, MU_CHUNKS + j : MU_CHUNKS + j + 1],
                in1=acc[j][:, cols],
                op0=MULT,
                op1=ADD,
            )

        def scale_y(j, cols):
            nc.vector.tensor_tensor(out=f_out[j][:, cols], in0=y_out[j][:, cols], in1=mu_all[:, cols], op=MULT)

        def add_f(j, cols):
            nc.vector.tensor_tensor(out=f_out[j][:, cols], in0=f_out[j][:, cols], in1=f_rows[j][:, cols], op=ADD)

        def store_chunk_ending_at(j):
            if j in chunk_ending_at:
                lo, hi, y_chunk, f_chunk = chunk_ending_at[j]
                nc.sync.dma_start(out=tile_rows(out_0, lo, hi), in_=y_chunk[:])
                nc.sync.dma_start(out=tile_rows(out_1, lo, hi), in_=f_chunk[:])

        whole = slice(0, B)
        pending = [(step, j) for j in range(LAST) for step in (scale_y, add_f)]

        def run_pending(at_most, newest_tile):
            for step, j in pending[:at_most]:
                if j <= newest_tile:
                    pending.remove((step, j))
                    step(j, whole)
                    if step is add_f:
                        store_chunk_ending_at(j)

        for j in range(HEAD):
            acc[j] = psum_bank(j, [P, B])
        turn(0)
        copy_out(0, 0)
        interleave(("x_prev", 0), X_PREV_VECTOR_COLS)
        copy_out(0, 1)
        turn(1)
        interleave(("x_prev", 1), X_PREV_VECTOR_COLS)
        copy_out(1, 0)
        copy_out(1, 1)
        for s in range(2):
            quantize(("x_prev", s))
            quantize(("v", s))
        for g in range(1, PASSES):
            load_k_rows("x", x, g)
        load_w_scales()
        load_w(W_CHUNKS[0])
        interleave(("x_prev", 2), X_PREV_VECTOR_COLS)
        sort_words(2)
        head_passes_v((0, 1), (0, 1))
        quantize(("x_prev", 2))
        interleave(("x_prev", 3), X_PREV_VECTOR_COLS)
        sort_words(3)
        turn_and_copy(2)
        head_passes_v((0, 1), (2,))
        quantize(("x_prev", 3))
        quantize(("v", 2))

        for j in range(2, HEAD):
            if j + 2 < HEAD:
                sort_words(j + 2)
            if j + 1 < HEAD:
                turn_and_copy(j + 1)
            interleave(("x", j - 2), X_VECTOR_COLS[j - 2])
            if j + 1 < HEAD:
                quantize(("v", j + 1))
            quantize(("x", j - 2))
            if j == 2:
                head_passes_v((0, 1), (3,))
            head_passes_v((j,), range(PASSES))

        load_v(6)
        load_rows("x_rows", x, X_ROW_CHUNKS[0], x_rows)
        load_v(7)
        load_w(W_CHUNKS[1])
        load_rows("f_rows", f, F_CHUNKS[0], f_rows)
        load_v(8)
        load_rows("x_rows", x, X_ROW_CHUNKS[1], x_rows)
        load_v(9)
        load_rows("f_rows", f, F_CHUNKS[1], f_rows)
        load_v(10)
        load_w(W_CHUNKS[2])
        load_v(11)
        load_rows("x_rows", x, X_ROW_CHUNKS[2], x_rows)
        load_v(12)
        load_rows("f_rows", f, F_CHUNKS[2], f_rows)
        for j in range(13, TILES):
            load_v(j)

        sort_words(HEAD)
        for j in range(HEAD):
            if j == NEXT_TURN_AT:
                turn_and_copy(HEAD)
                sort_words(HEAD + 1)
            if j > 0:
                finish_y(j - 1, whole)
                run_pending(1, j - 2)
            if j == NEXT_TURN_AT + 1:
                quantize(("v", HEAD))
            for g in range(PASSES):
                pass_w(j, g, False, g + 1 == PASSES)

        for j in range(HEAD, TILES):
            if j == HEAD:
                turn_and_copy(j + 1)
                sort_words(j + 2)
                sort_words(j + 3)
            elif j % 2 == 1 and j < LAST:
                turn_and_copy(j + 1)
                turn_and_copy(j + 2)
                if j + 3 < TILES:
                    sort_words(j + 3)
                    sort_words(j + 4)
            finish_y(j - 1, whole)
            run_pending(1, j - 2)
            if j < LAST:
                quantize(("v", j + 1))
            run_pending(2, j - 1)
            acc[j] = psum_bank(LATE_SUM_BANKS[(j - HEAD) % len(LATE_SUM_BANKS)], [P, B])
            for g in range(PASSES):
                pass_w(j, g, g == 0, False)
            for g in range(PASSES):
                pass_v(j, g, False, g + 1 == PASSES)

        assert not pending
        for step in (finish_y, scale_y, add_f):
            for half in range(2):
                step(LAST, slice(half * B // 2, (half + 1) * B // 2))
        store_chunk_ending_at(LAST)
